import numpy as np
import ml_dtypes


def mxq(x, axis, fmt="e4m3"):
    dtype, down = {"e4m3": (ml_dtypes.float8_e4m3fn, 7), "e5m2": (ml_dtypes.float8_e5m2, 14)}[fmt]
    v = np.moveaxis(np.asarray(x, np.float32).astype(ml_dtypes.bfloat16).astype(np.float64), axis, -1)
    blocks = v.reshape(v.shape[:-1] + (-1, 32))
    amax = np.abs(blocks).max(-1, keepdims=True)
    byte = np.maximum(np.where(amax > 0, np.frexp(amax)[1] - 1 + 127, 0) - down, 1)
    scale = np.exp2(byte - 127.0)
    codes = (blocks / scale).astype(np.float32).astype(dtype).astype(np.float64)
    return np.moveaxis((codes * scale).reshape(v.shape), -1, axis)


WIDE = False


def mx_kscale(k):
    if not WIDE:
        return np.ones(k)
    levels = np.array([10, -10, 5, -5, 0])
    if k % 512:
        return np.exp2(np.random.permutation(np.resize(levels, k // 32))).repeat(32)
    a = np.empty((k // 512, 16))
    for p in range(k // 512):
        a[p, :8] = np.random.permutation(np.resize(levels, 8))
        for g in range(8):
            far = levels[np.abs(levels - a[p, g]) >= 10]
            a[p, g + 8] = far[np.random.randint(len(far))]
    return np.exp2(a.ravel()).repeat(32)


BF16 = ml_dtypes.bfloat16


def bf(x):
    return np.asarray(x, np.float32).astype(BF16)


def f64(x):
    return np.asarray(x).astype(np.float64)


E2M1 = np.array([0.0, 0.5, 1.0, 1.5, 2.0, 3.0, 4.0, 6.0, -0.0, -0.5, -1.0, -1.5, -2.0, -3.0, -4.0, -6.0])


def pack_weight(w, fmt):
    k, n = w.shape
    w = f64(bf(w)).reshape(k // 32, 32, n)
    amax = np.abs(w).max(1)
    if fmt == "e4m3":
        byte = np.frexp(amax)[1] - 1 + 127 - 7
    else:
        mant, ex = np.frexp(amax / 6.0)
        byte = np.where(mant > 0.5, ex, ex - 1) + 127
    byte = np.clip(np.where(amax > 0, byte, 1), 1, 254)
    scaled = (w * np.exp2(127.0 - byte)[:, None, :]).reshape(k, n).astype(np.float32)
    by_word = np.ascontiguousarray(scaled.reshape(k // 512, 128, 4, n).transpose(0, 1, 3, 2))
    if fmt == "e4m3":
        words = by_word.astype(ml_dtypes.float8_e4m3fn).view(np.uint8)
    else:
        c = by_word.astype(ml_dtypes.float4_e2m1fn).view(np.uint8) & 0xF
        words = c[..., 0::2] | (c[..., 1::2] << 4)
    return np.ascontiguousarray(words), np.ascontiguousarray(byte.astype(np.uint8).reshape(k // 512, 16, n))


def unpack_weight(words, scales, fmt):
    g, p, n, _ = words.shape
    if fmt == "e4m3":
        vals = np.ascontiguousarray(words).view(ml_dtypes.float8_e4m3fn).astype(np.float64)
    else:
        nib = np.empty((g, p, n, 4), np.uint8)
        nib[..., 0::2] = words & 0xF
        nib[..., 1::2] = words >> 4
        vals = E2M1[nib]
    vals = vals * np.repeat(np.exp2(scales.astype(np.float64) - 127.0), 8, axis=1)[..., None]
    return vals.transpose(0, 1, 3, 2).reshape(g * 512, n)
def pack4(w):
    words, scales = pack_weight(w, "e2m1")
    return words.reshape(words.shape[0], 128, -1), scales


def unpack4(words, scales):
    return unpack_weight(words.reshape(words.shape[0], 128, -1, 2), scales, "e2m1")


def planes(Y):
    n, m = Y.shape
    b = f64(bf(Y)).reshape(n // 32, 32, m)
    amax = np.abs(b).max(1)
    byte = np.clip(np.where(amax > 0, np.frexp(amax)[1] - 1 + 127 - 7, 1), 1, 254)
    codes = (b * np.exp2(127.0 - byte)[:, None, :]).reshape(n, m).astype(np.float32).astype(ml_dtypes.float8_e4m3fn).view(np.uint8)
    words = codes.reshape(n // 512, 128, 4, m).transpose(0, 1, 3, 2)
    return np.ascontiguousarray(words), np.ascontiguousarray(byte.astype(np.uint8).reshape(n // 512, 16, m))


A, R = 1024, 2048
SPREAD = 1.4
REGION_SPREAD = 0.7

def setup_inputs():
    s = mx_kscale(A)
    infected = np.exp(SPREAD * np.random.randn(A, R) - SPREAD ** 2 / 2)
    infected_words, infected_scales = pack_weight(infected * s[:, None], "e4m3")
    contact = np.exp(SPREAD * np.random.randn(A, A) - SPREAD ** 2 / 2) / A
    rate = 0.8 * np.exp(REGION_SPREAD * np.random.randn(R))
    outside = 0.1 + 0.4 * np.random.rand(A)
    susceptibility = 0.3 + 0.7 * np.random.rand(A, R)
    return {"infected_words": infected_words, "infected_scales": infected_scales,
            "contact": bf(contact / s[:, None]), "rate": bf(rate),
            "outside": bf(outside), "susceptibility": bf(susceptibility)}

def reference(infected_words, infected_scales, contact, rate, outside, susceptibility):
    X = unpack_weight(infected_words, infected_scales, "e4m3")
    C = mxq(f64(contact), 0, "e4m3")
    L = C.T @ X
    y = (L * f64(rate)[None, :] + f64(outside)[:, None]) * f64(susceptibility)
    words, scales = planes(y.T)
    return y, words, scales

@@ -1,0 +1,263 @@
+from contextlib import ExitStack
+
+import concourse.mybir as mybir
+from concourse.masks import make_identity
+
+F32 = mybir.dt.float32
+BF16 = mybir.dt.bfloat16
+I32 = mybir.dt.int32
+U32 = mybir.dt.uint32
+U8 = mybir.dt.uint8
+FP8X4 = mybir.dt.float8_e4m3fn_x4
+COPY = mybir.ActivationFunctionType.Copy
+ADD = mybir.AluOpType.add
+MULT = mybir.AluOpType.mult
+
+A, R = 1024, 2048
+P = 128
+PACK = 4
+W = 512
+SUB = W // P
+PASSES = A // W
+HALVES = A // W
+CHUNKS = R // W
+BLOCKS = HALVES * CHUNKS
+V_COLS = 352
+FLOPS = 2 * A * A * R
+
+
+def tile_contact_infection_pressure_g6_kernel(
+    tc, infected_words, infected_scales, contact, rate, outside, susceptibility, out_0, out_1, out_2
+):
+    nc = tc.nc
+    with ExitStack() as ctx:
+        keep = ctx.enter_context(tc.tile_pool(name="keep", bufs=1))
+        work = ctx.enter_context(tc.tile_pool(name="work", bufs=2))
+        psum = ctx.enter_context(tc.psum_pool(name="psum", bufs=1))
+        ctx.enter_context(tc.manual_schedule())
+
+        x_scales = keep.tile([P, R], U8, name="x_scales", align_bytes=64)
+        nc.vector.memset(x_scales[:].bitcast(I32), 0)
+        for q in range(4):
+            nc.scalar.dma_start(
+                out=x_scales[32 * q : 32 * q + 4 * PASSES, :].bitcast(I32),
+                in_=infected_scales[:, 4 * q : 4 * q + 4, :].bitcast(I32),
+            )
+
+        c_raw, x_words, susc = {}, {}, {}
+
+        def load_c(h, g):
+            t = keep.tile([P, PACK, W], BF16, name="c_raw_%d_%d" % (h, g))
+            nc.sync.dma_start(
+                out=t[:], in_=contact[W * g : W * (g + 1), W * h : W * (h + 1)].rearrange("(p j) a -> p j a", j=PACK)
+            )
+            c_raw[h, g] = t
+
+        def load_x(c, gs):
+            t = keep.tile([P, len(gs), W], U32, name="x_words_%d_%d" % (c, gs[0]), align_bytes=64)
+            src = infected_words.rearrange("g p n t -> p g (n t)")
+            nc.sync.dma_start(
+                out=t[:].bitcast(I32),
+                in_=src[:, gs[0] : gs[-1] + 1, PACK * W * c : PACK * W * (c + 1)].bitcast(I32),
+            )
+            for n, g in enumerate(gs):
+                x_words[c, g] = t[:, n, :]
+
+        def load_s(h, cs):
+            t = keep.tile([P, SUB, len(cs) * W], BF16, name="susc_%d_%d" % (h, cs[0]))
+            nc.sync.dma_start(
+                out=t[:],
+                in_=susceptibility[W * h : W * (h + 1), W * cs[0] : W * (cs[-1] + 1)].rearrange("(i p) r -> p i r", p=P),
+            )
+            for n, c in enumerate(cs):
+                susc[h, c] = t[:, :, W * n : W * (n + 1)]
+
+        load_c(0, 0)
+        load_x(0, [0])
+        load_c(0, 1)
+        load_x(0, [1])
+        load_c(1, 0)
+        load_c(1, 1)
+        load_s(0, [0])
+        load_x(1, [0, 1])
+        load_s(0, [1])
+        load_x(2, [0, 1])
+        load_s(0, [2, 3])
+        load_x(3, [0, 1])
+        load_s(1, [0, 1])
+        load_s(1, [2, 3])
+
+        vec_rows = keep.tile([P, P], BF16, name="vec_rows")
+        nc.vector.memset(vec_rows[:], 0.0)
+        ident_bf = keep.tile([P, P], BF16, name="ident_bf")
+        make_identity(nc, ident_bf[:])
+        nc.gpsimd.dma_start(out=vec_rows[0 : R // P, :], in_=rate.rearrange("(c p) -> c p", p=P))
+        nc.gpsimd.dma_start(out=vec_rows[32 : 32 + A // P, :], in_=outside.rearrange("(c p) -> c p", p=P))
+        ident = keep.tile([P, P], F32, name="ident")
+        nc.scalar.activation(out=ident[:], in_=ident_bf[:], func=COPY)
+
+        c_codes, c_scales, c_grouped = {}, {}, {}
+
+        def interleave_c(h, g, eng, lo, hi):
+            if (h, g) not in c_grouped:
+                c_grouped[h, g] = keep.tile([P, W * PACK], BF16, name="c_grouped_%d_%d" % (h, g), align_bytes=64)
+            dst = c_grouped[h, g][:, PACK * lo : PACK * hi].rearrange("p (c i t) -> p c t i", i=4, t=PACK)
+            src = c_raw[h, g][:, :, lo:hi].rearrange("p t (c i) -> p c t i", i=4)
+            if eng == "v":
+                nc.vector.tensor_copy(out=dst, in_=src)
+            else:
+                nc.scalar.copy(out=dst, in_=src)
+
+        def quantize_c(h, g):
+            c_codes[h, g] = keep.tile([P, W], U32, name="c_codes_%d_%d" % (h, g), align_bytes=64)
+            c_scales[h, g] = keep.tile([P, W], U8, name="c_scales_%d_%d" % (h, g), align_bytes=64)
+            nc.vector.quantize_mx(out=c_codes[h, g][:].bitcast(FP8X4), scales=c_scales[h, g][:], in_=c_grouped[h, g][:])
+
+        interleave_c(0, 0, "v", 0, V_COLS)
+        interleave_c(0, 0, "s", V_COLS, W)
+        quantize_c(0, 0)
+        interleave_c(0, 1, "v", 0, V_COLS)
+        interleave_c(0, 1, "s", V_COLS, W)
+        vec_ps = psum.tile([P, P], BF16, name="vec_ps", tag="u")
+        nc.tensor.transpose(vec_ps[:], vec_rows[:], ident_bf[:])
+        cols = keep.tile([P, 64], F32, name="cols")
+        nc.scalar.copy(out=cols[:], in_=vec_ps[:, 0:64])
+        quantize_c(0, 1)
+        interleave_c(1, 0, "v", 0, W)
+        interleave_c(1, 1, "v", 0, W)
+        quantize_c(1, 0)
+        quantize_c(1, 1)
+
+        y_scales = keep.tile([P, A], U8, name="y_scales", align_bytes=64)
+        scaled, turned, y_tiles, rounded, grouped = {}, {}, {}, {}, {}
+
+        def multiply(b, j, g):
+            h, c = divmod(b, CHUNKS)
+            if g == 0:
+                scaled[b, j, "ps"] = psum.tile([P, W], F32, name="sums", tag="m%d" % j)
+            nc.tensor.matmul_mx(
+                out=scaled[b, j, "ps"][:],
+                lhsT=x_words[c, g][:, P * j : P * (j + 1)].bitcast(FP8X4),
+                lhsT_scale=x_scales[4 * g :, W * c + P * j : W * c + P * (j + 1)],
+                rhs=c_codes[h, g][:].bitcast(FP8X4),
+                rhs_scale=c_scales[h, g][:],
+                start=(g == 0),
+                stop=(g == PASSES - 1),
+            )
+
+        def scale(b, j):
+            c = b % CHUNKS
+            scaled[b, j] = work.tile([P, W], F32, name="scaled", tag="scaled%d" % j)
+            nc.scalar.activation(
+                out=scaled[b, j][:], in_=scaled[b, j, "ps"][:], func=COPY, scale=cols[:, SUB * c + j : SUB * c + j + 1]
+            )
+
+        def turn(b, i, js):
+            for j in js:
+                if j == 0:
+                    turned[b, i] = psum.tile([P, W], F32, name="turned", tag="t%d" % ((SUB * b + i) % 3))
+                nc.tensor.transpose(turned[b, i][:, P * j : P * (j + 1)], scaled[b, j][:, P * i : P * (i + 1)], ident[:])
+
+        def finish(b, i):
+            h, c = divmod(b, CHUNKS)
+            if i == 0:
+                y_tiles[b] = work.tile([P, SUB, W], F32, name="y", tag="y", bufs=6)
+            nc.vector.scalar_tensor_tensor(
+                out=y_tiles[b][:, i, :],
+                in0=turned[b, i][:],
+                scalar=cols[:, 32 + SUB * h + i : 32 + SUB * h + i + 1],
+                in1=susc[h, c][:, i, :],
+                op0=ADD,
+                op1=MULT,
+            )
+
+        def round_y(b, i, copy=nc.vector.tensor_copy):
+            rounded[b, i] = work.tile([P, W], BF16, name="rounded", tag="rounded%d" % i)
+            copy(
+                out=rounded[b, i][:].rearrange("a (u p e) -> a u p e", u=2, e=2),
+                in_=y_tiles[b][:, i, :].rearrange("a (p u e) -> a u p e", u=2, e=2),
+            )
+
+        def turn_words(b, subs, tag="u", copy=nc.scalar.copy):
+            if subs[0] == 0:
+                grouped[b] = work.tile([P, W * PACK], BF16, name="grouped", tag="grouped", align_bytes=64)
+            bank = psum.tile([P, len(subs), 2, P], F32, name="words_ps", tag=tag)
+            for n, i in enumerate(subs):
+                words = rounded[b, i][:].bitcast(F32)
+                for u in range(2):
+                    nc.tensor.transpose(bank[:, n, u, :], words[:, P * u : P * (u + 1)], ident[:])
+            dst = grouped[b][:].bitcast(F32)[:, 2 * P * subs[0] : 2 * P * (subs[-1] + 1)]
+            copy(out=dst.rearrange("p (n a u) -> p n a u", n=len(subs), u=2), in_=bank[:].rearrange("p n u a -> p n a u"))
+
+        def quantize_y(b, subs):
+            h, c = divmod(b, CHUNKS)
+            lo, hi = P * subs[0], P * (subs[-1] + 1)
+            codes = work.tile([P, hi - lo], U32, name="y_codes", tag="y_codes", bufs=4, align_bytes=64)
+            nc.vector.quantize_mx(
+                out=codes[:].bitcast(FP8X4),
+                scales=y_scales[4 * c :, W * h + lo : W * h + hi],
+                in_=grouped[b][:, PACK * lo : PACK * hi],
+            )
+            dst = out_1[c].rearrange("p m t -> p (m t)")[:, PACK * (W * h + lo) : PACK * (W * h + hi)]
+            nc.sync.dma_start(out=dst.bitcast(I32), in_=codes[:].bitcast(I32))
+
+        def store_y(b, subs):
+            h, c = divmod(b, CHUNKS)
+            rows = slice(W * h + P * subs[0], W * h + P * (subs[-1] + 1))
+            nc.sync.dma_start(
+                out=out_0[rows, W * c : W * (c + 1)].rearrange("(i p) r -> p i r", p=P),
+                in_=y_tiles[b][:, subs[0] : subs[-1] + 1, :],
+            )
+
+        last = BLOCKS - 1
+        for b in range(BLOCKS):
+            if b == 0:
+                for j in range(SUB):
+                    multiply(b, j, 0)
+            for j in range(SUB):
+                for g in range(PASSES):
+                    if b > 0 or g > 0:
+                        multiply(b, j, g)
+                scale(b, j)
+            if b > 0:
+                turn_words(b - 1, [0, 1])
+            turn(b, 0, [0, 1, 2])
+            turn(b, 1, [0, 1, 2])
+            turn(b, 0, [3])
+            turn(b, 1, [3])
+            finish(b, 0)
+            finish(b, 1)
+            turn(b, 2, range(SUB))
+            if b > 0:
+                turn_words(b - 1, [2, 3])
+            turn(b, 3, range(SUB))
+            if b < last:
+                round_y(b, 0)
+                finish(b, 2)
+                if b > 0:
+                    quantize_y(b - 1, [0, 1, 2, 3])
+                round_y(b, 1)
+                finish(b, 3)
+                store_y(b, [0, 1, 2, 3])
+                round_y(b, 2)
+                round_y(b, 3)
+
+        store_y(last, [0, 1])
+        round_y(last, 0, nc.scalar.copy)
+        finish(last, 2)
+        round_y(last, 1, nc.scalar.copy)
+        store_y(last, [2])
+        finish(last, 3)
+        store_y(last, [3])
+        quantize_y(last - 1, [0, 1, 2, 3])
+        round_y(last, 3)
+        round_y(last, 2, nc.scalar.copy)
+        turn_words(last, [0, 1], "m0")
+        turn_words(last, [2, 3], "m1", nc.vector.tensor_copy)
+        quantize_y(last, [0, 1])
+        quantize_y(last, [2, 3])
+
+        for q in range(4):
+            nc.scalar.dma_start(
+                out=out_2[:, 4 * q : 4 * q + 4, :].bitcast(I32), in_=y_scales[32 * q : 32 * q + 4 * CHUNKS, :].bitcast(I32)
+            )

@@ -77,13 +77,13 @@ def tile_contact_infection_pressure_g6_kernel(
         load_c(0, 1)
         load_x(0, [1])
         load_c(1, 0)
-        load_c(1, 1)
-        load_s(0, [0])
         load_x(1, [0, 1])
-        load_s(0, [1])
+        load_s(0, [0])
+        load_c(1, 1)
         load_x(2, [0, 1])
-        load_s(0, [2, 3])
+        load_s(0, [1])
         load_x(3, [0, 1])
+        load_s(0, [2, 3])
         load_s(1, [0, 1])
         load_s(1, [2, 3])
 
@@ -113,54 +113,87 @@ def tile_contact_infection_pressure_g6_kernel(
             c_scales[h, g] = keep.tile([P, W], U8, name="c_scales_%d_%d" % (h, g), align_bytes=64)
             nc.vector.quantize_mx(out=c_codes[h, g][:].bitcast(FP8X4), scales=c_scales[h, g][:], in_=c_grouped[h, g][:])
 
-        interleave_c(0, 0, "v", 0, V_COLS)
-        interleave_c(0, 0, "s", V_COLS, W)
-        quantize_c(0, 0)
-        interleave_c(0, 1, "v", 0, V_COLS)
-        interleave_c(0, 1, "s", V_COLS, W)
-        vec_ps = psum.tile([P, P], BF16, name="vec_ps", tag="u")
-        nc.tensor.transpose(vec_ps[:], vec_rows[:], ident_bf[:])
         cols = keep.tile([P, 64], F32, name="cols")
-        nc.scalar.copy(out=cols[:], in_=vec_ps[:, 0:64])
-        quantize_c(0, 1)
-        interleave_c(1, 0, "v", 0, W)
-        interleave_c(1, 1, "v", 0, W)
-        quantize_c(1, 0)
-        quantize_c(1, 1)
-
+        rate_cols = keep.tile([P, R // P], BF16, name="rate_cols")
+        rate_rows = [keep.tile([P, R // 2], BF16, name="rate_rows_%d" % n) for n in range(2)]
         y_scales = keep.tile([P, A], U8, name="y_scales", align_bytes=64)
-        scaled, turned, y_tiles, rounded, grouped = {}, {}, {}, {}, {}
+        sums, scaled, turned, y_tiles, rounded, grouped, y_codes = {}, {}, {}, {}, {}, {}, {}
 
-        def multiply(b, j, g):
-            h, c = divmod(b, CHUNKS)
-            if g == 0:
-                scaled[b, j, "ps"] = psum.tile([P, W], F32, name="sums", tag="m%d" % j)
+        def turn_vectors():
+            bank = psum.tile([P, P], BF16, name="vec_ps", tag="u0")
+            nc.tensor.transpose(bank[:], vec_rows[:], ident_bf[:])
+            nc.scalar.copy(out=cols[:], in_=bank[:, 0:64])
+            nc.scalar.copy(out=rate_cols[:], in_=bank[:, 0 : R // P])
+
+        def spread_rate(n, tag):
+            bank = psum.tile([P, R // 2], BF16, name="rate_ps", tag=tag)
+            for m in range(R // P // 2):
+                col = R // P // 2 * n + m
+                nc.tensor.transpose(
+                    bank[:, P * m : P * (m + 1)], rate_cols[:, col : col + 1].to_broadcast([P, P]), ident_bf[:]
+                )
+            nc.scalar.copy(out=rate_rows[n][:], in_=bank[:])
+
+        def x_operand(c, g, lo, hi):
+            return x_words[c, g][:, lo:hi].bitcast(FP8X4), x_scales[4 * g :, W * c + lo : W * c + hi]
+
+        def c_operand(h, g, lo, hi):
+            return c_codes[h, g][:, lo:hi].bitcast(FP8X4), c_scales[h, g][:, lo:hi]
+
+        def mx_pass(out, stationary, moving, g):
             nc.tensor.matmul_mx(
-                out=scaled[b, j, "ps"][:],
-                lhsT=x_words[c, g][:, P * j : P * (j + 1)].bitcast(FP8X4),
-                lhsT_scale=x_scales[4 * g :, W * c + P * j : W * c + P * (j + 1)],
-                rhs=c_codes[h, g][:].bitcast(FP8X4),
-                rhs_scale=c_scales[h, g][:],
+                out=out,
+                lhsT=stationary[0],
+                lhsT_scale=stationary[1],
+                rhs=moving[0],
+                rhs_scale=moving[1],
                 start=(g == 0),
                 stop=(g == PASSES - 1),
             )
 
-        def scale(b, j):
+        def multiply_direct(b, i):
+            h, c = divmod(b, CHUNKS)
+            sums[b, "d", i] = psum.tile([P, W], F32, name="sums_d", tag="a%d" % i)
+            for g in range(PASSES):
+                mx_pass(sums[b, "d", i][:], c_operand(h, g, P * i, P * (i + 1)), x_operand(c, g, 0, W), g)
+
+        def multiply_turned(b, j, g):
+            h, c = divmod(b, CHUNKS)
+            mx_pass(sums[b, "t", j], x_operand(c, g, P * j, P * (j + 1)), c_operand(h, g, W // 2, W), g)
+
+        def scale_turned(b, j):
             c = b % CHUNKS
-            scaled[b, j] = work.tile([P, W], F32, name="scaled", tag="scaled%d" % j)
+            scaled[b, j] = work.tile([P, W // 2], F32, name="scaled", tag="scaled%d" % j)
             nc.scalar.activation(
-                out=scaled[b, j][:], in_=scaled[b, j, "ps"][:], func=COPY, scale=cols[:, SUB * c + j : SUB * c + j + 1]
+                out=scaled[b, j][:], in_=sums[b, "t", j], func=COPY, scale=cols[:, SUB * c + j : SUB * c + j + 1]
             )
 
-        def turn(b, i, js):
-            for j in js:
-                if j == 0:
-                    turned[b, i] = psum.tile([P, W], F32, name="turned", tag="t%d" % ((SUB * b + i) % 3))
-                nc.tensor.transpose(turned[b, i][:, P * j : P * (j + 1)], scaled[b, j][:, P * i : P * (i + 1)], ident[:])
+        def multiply_pair(b, k):
+            bank = psum.tile([P, 2, W // 2], F32, name="sums_t", tag="b%d" % k)
+            for n in range(2):
+                sums[b, "t", 2 * k + n] = bank[:, n, :]
+                for g in range(PASSES):
+                    multiply_turned(b, 2 * k + n, g)
+            for n in range(2):
+                scale_turned(b, 2 * k + n)
+
+        def scale_direct(b, i):
+            c = b % CHUNKS
+            turned[b, i] = work.tile([P, W], F32, name="direct", tag="direct")
+            nc.vector.tensor_tensor(
+                out=turned[b, i][:], in0=sums[b, "d", i][:], in1=rate_rows[c // 2][:, W * (c % 2) : W * (c % 2 + 1)], op=MULT
+            )
+
+        def turn(b, i):
+            turned[b, i] = psum.tile([P, W], F32, name="turned", tag="t%d" % (i % 2))
+            for j in range(SUB):
+                nc.tensor.transpose(
+                    turned[b, i][:, P * j : P * (j + 1)], scaled[b, j][:, P * (i - 2) : P * (i - 1)], ident[:]
+                )
 
         def finish(b, i):
             h, c = divmod(b, CHUNKS)
-            if i == 0:
+            if b not in y_tiles:
                 y_tiles[b] = work.tile([P, SUB, W], F32, name="y", tag="y", bufs=6)
             nc.vector.scalar_tensor_tensor(
                 out=y_tiles[b][:, i, :],
@@ -171,91 +204,116 @@ def tile_contact_infection_pressure_g6_kernel(
                 op1=MULT,
             )
 
-        def round_y(b, i, copy=nc.vector.tensor_copy):
+        def round_y(b, i, copy):
             rounded[b, i] = work.tile([P, W], BF16, name="rounded", tag="rounded%d" % i)
             copy(
                 out=rounded[b, i][:].rearrange("a (u p e) -> a u p e", u=2, e=2),
                 in_=y_tiles[b][:, i, :].rearrange("a (p u e) -> a u p e", u=2, e=2),
             )
 
-        def turn_words(b, subs, tag="u", copy=nc.scalar.copy):
-            if subs[0] == 0:
+        def turn_words(b, subs, tag, copy):
+            if b not in grouped:
                 grouped[b] = work.tile([P, W * PACK], BF16, name="grouped", tag="grouped", align_bytes=64)
             bank = psum.tile([P, len(subs), 2, P], F32, name="words_ps", tag=tag)
             for n, i in enumerate(subs):
                 words = rounded[b, i][:].bitcast(F32)
                 for u in range(2):
                     nc.tensor.transpose(bank[:, n, u, :], words[:, P * u : P * (u + 1)], ident[:])
-            dst = grouped[b][:].bitcast(F32)[:, 2 * P * subs[0] : 2 * P * (subs[-1] + 1)]
-            copy(out=dst.rearrange("p (n a u) -> p n a u", n=len(subs), u=2), in_=bank[:].rearrange("p n u a -> p n a u"))
+            dst = grouped[b][:].bitcast(F32).rearrange("p (i a u) -> p i a u", i=SUB, u=2)
+            copy(out=dst[:, subs[0] : subs[-1] + 1 : 2, :, :], in_=bank[:].rearrange("p n u a -> p n a u"))
 
-        def quantize_y(b, subs):
+        def quantize_y(b, lo, hi):
             h, c = divmod(b, CHUNKS)
-            lo, hi = P * subs[0], P * (subs[-1] + 1)
-            codes = work.tile([P, hi - lo], U32, name="y_codes", tag="y_codes", bufs=4, align_bytes=64)
+            if b not in y_codes:
+                y_codes[b] = work.tile([P, W], U32, name="y_codes", tag="y_codes", bufs=4, align_bytes=64)
             nc.vector.quantize_mx(
-                out=codes[:].bitcast(FP8X4),
-                scales=y_scales[4 * c :, W * h + lo : W * h + hi],
-                in_=grouped[b][:, PACK * lo : PACK * hi],
+                out=y_codes[b][:, P * lo : P * hi].bitcast(FP8X4),
+                scales=y_scales[4 * c :, W * h + P * lo : W * h + P * hi],
+                in_=grouped[b][:, W * lo : W * hi],
             )
-            dst = out_1[c].rearrange("p m t -> p (m t)")[:, PACK * (W * h + lo) : PACK * (W * h + hi)]
-            nc.sync.dma_start(out=dst.bitcast(I32), in_=codes[:].bitcast(I32))
 
-        def store_y(b, subs):
+        def store_codes(b):
             h, c = divmod(b, CHUNKS)
-            rows = slice(W * h + P * subs[0], W * h + P * (subs[-1] + 1))
+            dst = out_1[c].rearrange("p m t -> p (m t)")[:, PACK * W * h : PACK * W * (h + 1)]
+            nc.sync.dma_start(out=dst.bitcast(I32), in_=y_codes[b][:].bitcast(I32))
+
+        def store_y(b, lo, hi):
+            h, c = divmod(b, CHUNKS)
             nc.sync.dma_start(
-                out=out_0[rows, W * c : W * (c + 1)].rearrange("(i p) r -> p i r", p=P),
-                in_=y_tiles[b][:, subs[0] : subs[-1] + 1, :],
+                out=out_0[W * h + P * lo : W * h + P * hi, W * c : W * (c + 1)].rearrange("(i p) r -> p i r", p=P),
+                in_=y_tiles[b][:, lo:hi, :],
             )
 
-        last = BLOCKS - 1
-        for b in range(BLOCKS):
-            if b == 0:
-                for j in range(SUB):
-                    multiply(b, j, 0)
-            for j in range(SUB):
-                for g in range(PASSES):
-                    if b > 0 or g > 0:
-                        multiply(b, j, g)
-                scale(b, j)
-            if b > 0:
-                turn_words(b - 1, [0, 1])
-            turn(b, 0, [0, 1, 2])
-            turn(b, 1, [0, 1, 2])
-            turn(b, 0, [3])
-            turn(b, 1, [3])
-            finish(b, 0)
-            finish(b, 1)
-            turn(b, 2, range(SUB))
-            if b > 0:
-                turn_words(b - 1, [2, 3])
-            turn(b, 3, range(SUB))
-            if b < last:
-                round_y(b, 0)
-                finish(b, 2)
-                if b > 0:
-                    quantize_y(b - 1, [0, 1, 2, 3])
-                round_y(b, 1)
-                finish(b, 3)
-                store_y(b, [0, 1, 2, 3])
-                round_y(b, 2)
-                round_y(b, 3)
+        on_vector, on_scalar = nc.vector.tensor_copy, nc.scalar.copy
 
-        store_y(last, [0, 1])
-        round_y(last, 0, nc.scalar.copy)
-        finish(last, 2)
-        round_y(last, 1, nc.scalar.copy)
-        store_y(last, [2])
-        finish(last, 3)
-        store_y(last, [3])
-        quantize_y(last - 1, [0, 1, 2, 3])
-        round_y(last, 3)
-        round_y(last, 2, nc.scalar.copy)
-        turn_words(last, [0, 1], "m0")
-        turn_words(last, [2, 3], "m1", nc.vector.tensor_copy)
-        quantize_y(last, [0, 1])
-        quantize_y(last, [2, 3])
+        interleave_c(0, 0, "v", 0, V_COLS)
+        interleave_c(0, 0, "s", V_COLS, W)
+        quantize_c(0, 0)
+        interleave_c(0, 1, "v", 0, V_COLS)
+        interleave_c(0, 1, "s", V_COLS, W)
+        for j, tag in enumerate(["a0", "a1", "b0", "b1"]):
+            bank = psum.tile([P, W // 2], F32, name="sums_0", tag=tag)
+            sums[0, "t", j] = bank[:]
+            multiply_turned(0, j, 0)
+        turn_vectors()
+        quantize_c(0, 1)
+        for j in range(SUB):
+            multiply_turned(0, j, 1)
+        scale_turned(0, 0)
+        scale_turned(0, 1)
+        spread_rate(0, "u1")
+        scale_turned(0, 2)
+        scale_turned(0, 3)
+        interleave_c(1, 0, "v", 0, W)
+
+        last = 2 * BLOCKS - 1
+        for s in range(last + 1):
+            b, k = divmod(s, 2)
+            b1, k1 = divmod(s - 1, 2)
+            multiply_direct(b, k)
+            if b + 1 < BLOCKS:
+                multiply_pair(b + 1, k)
+            turn(b, 2 + k)
+            scale_direct(b, k)
+            if s >= 1:
+                round_y(b1, k1, on_scalar)
+            if s == 0:
+                spread_rate(1, "u0")
+            if s >= 2:
+                turn_words(b - 1, [k, 2 + k], "u%d" % k, on_scalar)
+            if s < SUB:
+                interleave_c(1, 1, "s", P * s, P * (s + 1))
+            if s == 0:
+                quantize_c(1, 0)
+            if s == SUB:
+                quantize_c(1, 1)
+            if s >= 4 and k == 0:
+                quantize_y(b - 2, 0, SUB)
+                store_codes(b - 2)
+            if s >= 1:
+                round_y(b1, 2 + k1, on_vector if (k == 1 and s < last) else on_scalar)
+            finish(b, k)
+            if s == last:
+                store_y(b, 0, 2)
+            finish(b, 2 + k)
+            if s == last:
+                store_y(b, 2, SUB)
+            elif k == 1:
+                store_y(b, 0, SUB)
+
+        b = BLOCKS - 1
+        turn_words(b, [0, 2], "u0", on_scalar)
+        round_y(b, 1, on_scalar)
+        quantize_y(b - 1, 0, SUB)
+        store_codes(b - 1)
+        round_y(b, 3, on_vector)
+        turn_words(b, [1], "u1", on_scalar)
+        quantize_y(b, 0, 1)
+        quantize_y(b, 2, 3)
+        turn_words(b, [3], "t0", on_vector)
+        quantize_y(b, 1, 2)
+        quantize_y(b, 3, 4)
+        store_codes(b)
 
         for q in range(4):
             nc.scalar.dma_start(

@@ -36,13 +36,10 @@ def tile_contact_infection_pressure_g6_kernel(
         psum = ctx.enter_context(tc.psum_pool(name="psum", bufs=1))
         ctx.enter_context(tc.manual_schedule())
 
+        vec_rows = keep.tile([P, P], BF16, name="vec_rows")
+        nc.vector.memset(vec_rows[:], 0.0)
         x_scales = keep.tile([P, R], U8, name="x_scales", align_bytes=64)
         nc.vector.memset(x_scales[:].bitcast(I32), 0)
-        for q in range(4):
-            nc.scalar.dma_start(
-                out=x_scales[32 * q : 32 * q + 4 * PASSES, :].bitcast(I32),
-                in_=infected_scales[:, 4 * q : 4 * q + 4, :].bitcast(I32),
-            )
 
         c_raw, x_words, susc = {}, {}, {}
 
@@ -63,36 +60,39 @@ def tile_contact_infection_pressure_g6_kernel(
             for n, g in enumerate(gs):
                 x_words[c, g] = t[:, n, :]
 
-        def load_s(h, cs):
-            t = keep.tile([P, SUB, len(cs) * W], BF16, name="susc_%d_%d" % (h, cs[0]))
-            nc.sync.dma_start(
-                out=t[:],
-                in_=susceptibility[W * h : W * (h + 1), W * cs[0] : W * (cs[-1] + 1)].rearrange("(i p) r -> p i r", p=P),
-            )
+        def load_s(h, k, cs):
+            t = keep.tile([P, 2, len(cs) * W], BF16, name="susc_%d_%d_%d" % (h, k, cs[0]))
+            rows = susceptibility[W * h : W * (h + 1), W * cs[0] : W * (cs[-1] + 1)].rearrange("(i p) r -> p i r", p=P)
+            nc.sync.dma_start(out=t[:], in_=rows[:, k::2, :])
             for n, c in enumerate(cs):
-                susc[h, c] = t[:, :, W * n : W * (n + 1)]
+                susc[h, c, k] = t[:, 0, W * n : W * (n + 1)]
+                susc[h, c, 2 + k] = t[:, 1, W * n : W * (n + 1)]
 
         load_c(0, 0)
-        load_x(0, [0])
+        nc.sync.dma_start(out=vec_rows[0 : R // P, :], in_=rate.rearrange("(c p) -> c p", p=P))
+        nc.sync.dma_start(out=vec_rows[32 : 32 + A // P, :], in_=outside.rearrange("(c p) -> c p", p=P))
         load_c(0, 1)
-        load_x(0, [1])
+        for q in range(4):
+            nc.sync.dma_start(
+                out=x_scales[32 * q : 32 * q + 4 * PASSES, :].bitcast(I32),
+                in_=infected_scales[:, 4 * q : 4 * q + 4, :].bitcast(I32),
+            )
+
+        load_x(0, [0, 1])
         load_c(1, 0)
         load_x(1, [0, 1])
-        load_s(0, [0])
-        load_c(1, 1)
+        load_s(0, 0, [0, 1])
+        load_s(0, 1, [0, 1])
         load_x(2, [0, 1])
-        load_s(0, [1])
+        load_c(1, 1)
         load_x(3, [0, 1])
-        load_s(0, [2, 3])
-        load_s(1, [0, 1])
-        load_s(1, [2, 3])
+        load_s(0, 0, [2, 3])
+        load_s(0, 1, [2, 3])
+        load_s(1, 0, [0, 1, 2, 3])
+        load_s(1, 1, [0, 1, 2, 3])
 
-        vec_rows = keep.tile([P, P], BF16, name="vec_rows")
-        nc.vector.memset(vec_rows[:], 0.0)
         ident_bf = keep.tile([P, P], BF16, name="ident_bf")
         make_identity(nc, ident_bf[:])
-        nc.gpsimd.dma_start(out=vec_rows[0 : R // P, :], in_=rate.rearrange("(c p) -> c p", p=P))
-        nc.gpsimd.dma_start(out=vec_rows[32 : 32 + A // P, :], in_=outside.rearrange("(c p) -> c p", p=P))
         ident = keep.tile([P, P], F32, name="ident")
         nc.scalar.activation(out=ident[:], in_=ident_bf[:], func=COPY)
 
@@ -115,7 +115,7 @@ def tile_contact_infection_pressure_g6_kernel(
 
         cols = keep.tile([P, 64], F32, name="cols")
         rate_cols = keep.tile([P, R // P], BF16, name="rate_cols")
-        rate_rows = [keep.tile([P, R // 2], BF16, name="rate_rows_%d" % n) for n in range(2)]
+        rate_rows = [keep.tile([P, 2 * W], BF16, name="rate_rows_%d" % n) for n in range(CHUNKS // 2)]
         y_scales = keep.tile([P, A], U8, name="y_scales", align_bytes=64)
         sums, scaled, turned, y_tiles, rounded, grouped, y_codes = {}, {}, {}, {}, {}, {}, {}
 
@@ -126,9 +126,9 @@ def tile_contact_infection_pressure_g6_kernel(
             nc.scalar.copy(out=rate_cols[:], in_=bank[:, 0 : R // P])
 
         def spread_rate(n, tag):
-            bank = psum.tile([P, R // 2], BF16, name="rate_ps", tag=tag)
-            for m in range(R // P // 2):
-                col = R // P // 2 * n + m
+            bank = psum.tile([P, 2 * W], BF16, name="rate_ps", tag=tag)
+            for m in range(2 * SUB):
+                col = 2 * SUB * n + m
                 nc.tensor.transpose(
                     bank[:, P * m : P * (m + 1)], rate_cols[:, col : col + 1].to_broadcast([P, P]), ident_bf[:]
                 )
@@ -194,12 +194,13 @@ def tile_contact_infection_pressure_g6_kernel(
         def finish(b, i):
             h, c = divmod(b, CHUNKS)
             if b not in y_tiles:
-                y_tiles[b] = work.tile([P, SUB, W], F32, name="y", tag="y", bufs=6)
+                wide = work.tile([P, SUB, 2 * W], F32, name="y", tag="y", bufs=3)
+                y_tiles[b], y_tiles[b + 1], y_tiles[b, b + 1] = wide[:, :, :W], wide[:, :, W:], wide
             nc.vector.scalar_tensor_tensor(
                 out=y_tiles[b][:, i, :],
                 in0=turned[b, i][:],
                 scalar=cols[:, 32 + SUB * h + i : 32 + SUB * h + i + 1],
-                in1=susc[h, c][:, i, :],
+                in1=susc[h, c, i],
                 op0=ADD,
                 op1=MULT,
             )
@@ -232,88 +233,90 @@ def tile_contact_infection_pressure_g6_kernel(
                 in_=grouped[b][:, W * lo : W * hi],
             )
 
-        def store_codes(b):
+        def store_codes(b, lo, hi):
             h, c = divmod(b, CHUNKS)
-            dst = out_1[c].rearrange("p m t -> p (m t)")[:, PACK * W * h : PACK * W * (h + 1)]
-            nc.sync.dma_start(out=dst.bitcast(I32), in_=y_codes[b][:].bitcast(I32))
+            dst = out_1[c].rearrange("p m t -> p (m t)")[:, PACK * (W * h + P * lo) : PACK * (W * h + P * hi)]
+            nc.sync.dma_start(out=dst.bitcast(I32), in_=y_codes[b][:, P * lo : P * hi].bitcast(I32))
 
-        def store_y(b, lo, hi):
-            h, c = divmod(b, CHUNKS)
-            nc.sync.dma_start(
-                out=out_0[W * h + P * lo : W * h + P * hi, W * c : W * (c + 1)].rearrange("(i p) r -> p i r", p=P),
-                in_=y_tiles[b][:, lo:hi, :],
-            )
+        def store_y(first, last_b, subs):
+            h, c = divmod(first, CHUNKS)
+            dst = out_0[W * h : W * (h + 1), W * c : W * (c + 1 + last_b - first)].rearrange("(i p) r -> p i r", p=P)
+            src = y_tiles[first] if first == last_b else y_tiles[first, last_b]
+            nc.sync.dma_start(out=dst[:, subs, :], in_=src[:, subs, :])
+
+        def on_gpsimd(out, in_):
+            nc.gpsimd.tensor_scalar(out=out, in0=in_, scalar1=1.0, scalar2=0.0, op0=MULT, op1=ADD)
 
         on_vector, on_scalar = nc.vector.tensor_copy, nc.scalar.copy
 
         interleave_c(0, 0, "v", 0, V_COLS)
         interleave_c(0, 0, "s", V_COLS, W)
+        turn_vectors()
         quantize_c(0, 0)
         interleave_c(0, 1, "v", 0, V_COLS)
         interleave_c(0, 1, "s", V_COLS, W)
-        for j, tag in enumerate(["a0", "a1", "b0", "b1"]):
+        spread_rate(0, "u1")
+        spread_rate(1, "t1")
+        quantize_c(0, 1)
+        multiply_direct(0, 0)
+        for j, tag in enumerate(["b0", "b1", "t0", "t1"]):
             bank = psum.tile([P, W // 2], F32, name="sums_0", tag=tag)
             sums[0, "t", j] = bank[:]
-            multiply_turned(0, j, 0)
-        turn_vectors()
-        quantize_c(0, 1)
-        for j in range(SUB):
-            multiply_turned(0, j, 1)
-        scale_turned(0, 0)
-        scale_turned(0, 1)
-        spread_rate(0, "u1")
-        scale_turned(0, 2)
-        scale_turned(0, 3)
+            for g in range(PASSES):
+                multiply_turned(0, j, g)
+            scale_turned(0, j)
+        scale_direct(0, 0)
         interleave_c(1, 0, "v", 0, W)
+
+        def store_pair(b, k):
+            if b >= 4:
+                store_y(b, b, slice(k, SUB, 2))
+            elif b % 2 == 1:
+                store_y(b - 1, b, slice(k, SUB, 2))
 
         last = 2 * BLOCKS - 1
         for s in range(last + 1):
             b, k = divmod(s, 2)
             b1, k1 = divmod(s - 1, 2)
-            multiply_direct(b, k)
+            if s < last:
+                multiply_direct(*divmod(s + 1, 2))
             if b + 1 < BLOCKS:
                 multiply_pair(b + 1, k)
+            if s > 0:
+                scale_direct(b, k)
+                finish(b1, 2 + k1)
+                store_pair(b1, k1)
+                round_y(b1, 2 + k1, on_scalar)
             turn(b, 2 + k)
-            scale_direct(b, k)
-            if s >= 1:
-                round_y(b1, k1, on_scalar)
-            if s == 0:
-                spread_rate(1, "u0")
             if s >= 2:
                 turn_words(b - 1, [k, 2 + k], "u%d" % k, on_scalar)
-            if s < SUB:
-                interleave_c(1, 1, "s", P * s, P * (s + 1))
-            if s == 0:
-                quantize_c(1, 0)
-            if s == SUB:
-                quantize_c(1, 1)
+            if s == 3:
+                interleave_c(1, 1, "v", 0, W // 2)
+            if s in (3, 4):
+                interleave_c(1, 1, "s", P * (s - 1), P * s)
+            if s in (1, 5):
+                quantize_c(1, s // 4)
             if s >= 4 and k == 0:
                 quantize_y(b - 2, 0, SUB)
-                store_codes(b - 2)
-            if s >= 1:
-                round_y(b1, 2 + k1, on_vector if (k == 1 and s < last) else on_scalar)
+                store_codes(b - 2, 0, SUB)
             finish(b, k)
-            if s == last:
-                store_y(b, 0, 2)
-            finish(b, 2 + k)
-            if s == last:
-                store_y(b, 2, SUB)
-            elif k == 1:
-                store_y(b, 0, SUB)
+            round_y(b, k, on_gpsimd)
 
         b = BLOCKS - 1
+        store_y(b, b, slice(1, 2))
+        finish(b, 3)
+        store_y(b, b, slice(3, 4))
         turn_words(b, [0, 2], "u0", on_scalar)
-        round_y(b, 1, on_scalar)
-        quantize_y(b - 1, 0, SUB)
-        store_codes(b - 1)
         round_y(b, 3, on_vector)
         turn_words(b, [1], "u1", on_scalar)
-        quantize_y(b, 0, 1)
+        turn_words(b, [3], "t0", on_scalar)
+        quantize_y(b - 1, 0, SUB)
+        store_codes(b - 1, 0, SUB)
+        quantize_y(b, 0, 2)
+        store_codes(b, 0, 2)
         quantize_y(b, 2, 3)
-        turn_words(b, [3], "t0", on_vector)
-        quantize_y(b, 1, 2)
-        quantize_y(b, 3, 4)
-        store_codes(b)
+        quantize_y(b, 3, SUB)
+        store_codes(b, 2, SUB)
 
         for q in range(4):
             nc.scalar.dma_start(

@@ -70,7 +70,6 @@ def tile_contact_infection_pressure_g6_kernel(
 
         load_c(0, 0)
         nc.sync.dma_start(out=vec_rows[0 : R // P, :], in_=rate.rearrange("(c p) -> c p", p=P))
-        nc.sync.dma_start(out=vec_rows[32 : 32 + A // P, :], in_=outside.rearrange("(c p) -> c p", p=P))
         load_c(0, 1)
         for q in range(4):
             nc.sync.dma_start(
@@ -93,6 +92,9 @@ def tile_contact_infection_pressure_g6_kernel(
 
         ident_bf = keep.tile([P, P], BF16, name="ident_bf")
         make_identity(nc, ident_bf[:])
+        outside_rows = keep.tile([P, P], BF16, name="outside_rows")
+        nc.gpsimd.memset(outside_rows[:], 0.0)
+        nc.gpsimd.dma_start(out=outside_rows[0 : A // P, :], in_=outside.rearrange("(c p) -> c p", p=P))
         ident = keep.tile([P, P], F32, name="ident")
         nc.scalar.activation(out=ident[:], in_=ident_bf[:], func=COPY)
 
@@ -113,7 +115,8 @@ def tile_contact_infection_pressure_g6_kernel(
             c_scales[h, g] = keep.tile([P, W], U8, name="c_scales_%d_%d" % (h, g), align_bytes=64)
             nc.vector.quantize_mx(out=c_codes[h, g][:].bitcast(FP8X4), scales=c_scales[h, g][:], in_=c_grouped[h, g][:])
 
-        cols = keep.tile([P, 64], F32, name="cols")
+        cols = keep.tile([P, R // P], F32, name="cols")
+        outside_cols = keep.tile([P, A // P], F32, name="outside_cols")
         rate_cols = keep.tile([P, R // P], BF16, name="rate_cols")
         rate_rows = [keep.tile([P, 2 * W], BF16, name="rate_rows_%d" % n) for n in range(CHUNKS // 2)]
         y_scales = keep.tile([P, A], U8, name="y_scales", align_bytes=64)
@@ -122,8 +125,13 @@ def tile_contact_infection_pressure_g6_kernel(
         def turn_vectors():
             bank = psum.tile([P, P], BF16, name="vec_ps", tag="u0")
             nc.tensor.transpose(bank[:], vec_rows[:], ident_bf[:])
-            nc.scalar.copy(out=cols[:], in_=bank[:, 0:64])
+            nc.scalar.copy(out=cols[:], in_=bank[:, 0 : R // P])
             nc.scalar.copy(out=rate_cols[:], in_=bank[:, 0 : R // P])
+
+        def turn_outside():
+            bank = psum.tile([P, P], BF16, name="outside_ps", tag="u0")
+            nc.tensor.transpose(bank[:], outside_rows[:], ident_bf[:])
+            nc.scalar.copy(out=outside_cols[:], in_=bank[:, 0 : A // P])
 
         def spread_rate(n, tag):
             bank = psum.tile([P, 2 * W], BF16, name="rate_ps", tag=tag)
@@ -199,11 +207,24 @@ def tile_contact_infection_pressure_g6_kernel(
             nc.vector.scalar_tensor_tensor(
                 out=y_tiles[b][:, i, :],
                 in0=turned[b, i][:],
-                scalar=cols[:, 32 + SUB * h + i : 32 + SUB * h + i + 1],
+                scalar=outside_cols[:, SUB * h + i : SUB * h + i + 1],
                 in1=susc[h, c, i],
                 op0=ADD,
                 op1=MULT,
             )
+
+        def finish_rounded(b, i):
+            h, c = divmod(b, CHUNKS)
+            rounded[b, i] = work.tile([P, W], BF16, name="rounded", tag="rounded%d" % i)
+            for u in range(2):
+                nc.vector.scalar_tensor_tensor(
+                    out=rounded[b, i][:].rearrange("a (u p e) -> a u p e", u=2, e=2)[:, u],
+                    in0=turned[b, i][:].rearrange("a (p u e) -> a u p e", u=2, e=2)[:, u],
+                    scalar=outside_cols[:, SUB * h + i : SUB * h + i + 1],
+                    in1=susc[h, c, i].rearrange("a (p u e) -> a u p e", u=2, e=2)[:, u],
+                    op0=ADD,
+                    op1=MULT,
+                )
 
         def round_y(b, i, copy):
             rounded[b, i] = work.tile([P, W], BF16, name="rounded", tag="rounded%d" % i)
@@ -214,7 +235,7 @@ def tile_contact_infection_pressure_g6_kernel(
 
         def turn_words(b, subs, tag, copy):
             if b not in grouped:
-                grouped[b] = work.tile([P, W * PACK], BF16, name="grouped", tag="grouped", align_bytes=64)
+                grouped[b] = work.tile([P, W * PACK], BF16, name="grouped", tag="grouped", bufs=3, align_bytes=64)
             bank = psum.tile([P, len(subs), 2, P], F32, name="words_ps", tag=tag)
             for n, i in enumerate(subs):
                 words = rounded[b, i][:].bitcast(F32)
@@ -257,6 +278,7 @@ def tile_contact_infection_pressure_g6_kernel(
         interleave_c(0, 1, "s", V_COLS, W)
         spread_rate(0, "u1")
         spread_rate(1, "t1")
+        turn_outside()
         quantize_c(0, 1)
         multiply_direct(0, 0)
         for j, tag in enumerate(["b0", "b1", "t0", "t1"]):
@@ -267,6 +289,7 @@ def tile_contact_infection_pressure_g6_kernel(
             scale_turned(0, j)
         scale_direct(0, 0)
         interleave_c(1, 0, "v", 0, W)
+        quantize_c(1, 0)
 
         def store_pair(b, k):
             if b >= 4:
@@ -275,11 +298,10 @@ def tile_contact_infection_pressure_g6_kernel(
                 store_y(b - 1, b, slice(k, SUB, 2))
 
         last = 2 * BLOCKS - 1
-        for s in range(last + 1):
+        for s in range(last):
             b, k = divmod(s, 2)
             b1, k1 = divmod(s - 1, 2)
-            if s < last:
-                multiply_direct(*divmod(s + 1, 2))
+            multiply_direct(*divmod(s + 1, 2))
             if b + 1 < BLOCKS:
                 multiply_pair(b + 1, k)
             if s > 0:
@@ -290,33 +312,42 @@ def tile_contact_infection_pressure_g6_kernel(
             turn(b, 2 + k)
             if s >= 2:
                 turn_words(b - 1, [k, 2 + k], "u%d" % k, on_scalar)
-            if s == 3:
+            if s == 4:
                 interleave_c(1, 1, "v", 0, W // 2)
-            if s in (3, 4):
-                interleave_c(1, 1, "s", P * (s - 1), P * s)
-            if s in (1, 5):
-                quantize_c(1, s // 4)
-            if s >= 4 and k == 0:
+            if s in (2, 3):
+                interleave_c(1, 1, "s", P * s, P * (s + 1))
+            if s == 5:
+                quantize_c(1, 1)
+            if s >= 5 and k == 1:
                 quantize_y(b - 2, 0, SUB)
                 store_codes(b - 2, 0, SUB)
             finish(b, k)
             round_y(b, k, on_gpsimd)
 
         b = BLOCKS - 1
-        store_y(b, b, slice(1, 2))
+        turn(b, 3)
+        finish(b, 2)
+        store_pair(b, 0)
+        round_y(b, 2, on_scalar)
+        turn_words(b - 1, [1, 3], "u1", on_scalar)
+        scale_direct(b, 1)
         finish(b, 3)
         store_y(b, b, slice(3, 4))
+        round_y(b, 3, on_scalar)
         turn_words(b, [0, 2], "u0", on_scalar)
-        round_y(b, 3, on_vector)
-        turn_words(b, [1], "u1", on_scalar)
-        turn_words(b, [3], "t0", on_scalar)
+        finish_rounded(b, 1)
+        finish(b, 1)
+        store_y(b, b, slice(1, 2))
+        turn_words(b, [1, 3], "u1", on_scalar)
+        quantize_y(b - 2, 0, SUB)
+        store_codes(b - 2, 0, SUB)
         quantize_y(b - 1, 0, SUB)
         store_codes(b - 1, 0, SUB)
-        quantize_y(b, 0, 2)
-        store_codes(b, 0, 2)
+        quantize_y(b, 0, 1)
         quantize_y(b, 2, 3)
-        quantize_y(b, 3, SUB)
-        store_codes(b, 2, SUB)
+        quantize_y(b, 1, 2)
+        quantize_y(b, 3, 4)
+        store_codes(b, 0, SUB)
 
         for q in range(4):
             nc.scalar.dma_start(

@@ -16,13 +16,17 @@ MULT = mybir.AluOpType.mult
 A, R = 1024, 2048
 P = 128
 PACK = 4
+QUADRANTS, QUADRANT = 4, 32
+SCALE_ROWS = 4
 W = 512
-SUB = W // P
+STRIPS = W // P
+DIRECT = STRIPS // 2
 PASSES = A // W
 HALVES = A // W
 CHUNKS = R // W
 BLOCKS = HALVES * CHUNKS
 V_COLS = 352
+Y_RUNS = [[b, b + 1] for b in range(0, CHUNKS, 2)] + [[b] for b in range(CHUNKS, BLOCKS)]
 FLOPS = 2 * A * A * R
 
 
@@ -36,114 +40,112 @@ def tile_contact_infection_pressure_g6_kernel(
         psum = ctx.enter_context(tc.psum_pool(name="psum", bufs=1))
         ctx.enter_context(tc.manual_schedule())
 
-        vec_rows = keep.tile([P, P], BF16, name="vec_rows")
-        nc.vector.memset(vec_rows[:], 0.0)
+        rate_rows = keep.tile([P, P], BF16, name="rate_rows")
+        nc.vector.memset(rate_rows[:], 0.0)
         x_scales = keep.tile([P, R], U8, name="x_scales", align_bytes=64)
         nc.vector.memset(x_scales[:].bitcast(I32), 0)
 
         c_raw, x_words, susc = {}, {}, {}
 
-        def load_c(h, g):
-            t = keep.tile([P, PACK, W], BF16, name="c_raw_%d_%d" % (h, g))
-            nc.sync.dma_start(
-                out=t[:], in_=contact[W * g : W * (g + 1), W * h : W * (h + 1)].rearrange("(p j) a -> p j a", j=PACK)
-            )
-            c_raw[h, g] = t
+        def load_c(g):
+            t = keep.tile([P, PACK, A], BF16, name="c_raw_%d" % g)
+            nc.sync.dma_start(out=t[:], in_=contact[W * g : W * (g + 1), :].rearrange("(p j) a -> p j a", j=PACK))
+            for h in range(HALVES):
+                c_raw[h, g] = t[:, :, W * h : W * (h + 1)]
 
-        def load_x(c, gs):
-            t = keep.tile([P, len(gs), W], U32, name="x_words_%d_%d" % (c, gs[0]), align_bytes=64)
-            src = infected_words.rearrange("g p n t -> p g (n t)")
-            nc.sync.dma_start(
-                out=t[:].bitcast(I32),
-                in_=src[:, gs[0] : gs[-1] + 1, PACK * W * c : PACK * W * (c + 1)].bitcast(I32),
-            )
-            for n, g in enumerate(gs):
-                x_words[c, g] = t[:, n, :]
+        def load_x(chunks):
+            t = keep.tile([P, PASSES, len(chunks) * W], U32, name="x_words_%d" % chunks[0], align_bytes=64)
+            src = infected_words.rearrange("g p n t -> p g (n t)")[:, :, PACK * W * chunks[0] : PACK * W * (chunks[-1] + 1)]
+            nc.sync.dma_start(out=t[:].bitcast(I32), in_=src.bitcast(I32))
+            for g in range(PASSES):
+                for n, c in enumerate(chunks):
+                    x_words[c, g] = t[:, g, W * n : W * (n + 1)]
 
-        def load_s(h, k, cs):
-            t = keep.tile([P, 2, len(cs) * W], BF16, name="susc_%d_%d_%d" % (h, k, cs[0]))
-            rows = susceptibility[W * h : W * (h + 1), W * cs[0] : W * (cs[-1] + 1)].rearrange("(i p) r -> p i r", p=P)
-            nc.sync.dma_start(out=t[:], in_=rows[:, k::2, :])
-            for n, c in enumerate(cs):
+        def load_susc(h, k, chunks):
+            t = keep.tile([P, 2, len(chunks) * W], BF16, name="susc_%d_%d_%d" % (h, k, chunks[0]))
+            rows = susceptibility[W * h : W * (h + 1), W * chunks[0] : W * (chunks[-1] + 1)]
+            nc.sync.dma_start(out=t[:], in_=rows.rearrange("(i p) r -> p i r", p=P)[:, k::DIRECT, :])
+            for n, c in enumerate(chunks):
                 susc[h, c, k] = t[:, 0, W * n : W * (n + 1)]
-                susc[h, c, 2 + k] = t[:, 1, W * n : W * (n + 1)]
+                susc[h, c, DIRECT + k] = t[:, 1, W * n : W * (n + 1)]
 
-        load_c(0, 0)
-        nc.sync.dma_start(out=vec_rows[0 : R // P, :], in_=rate.rearrange("(c p) -> c p", p=P))
-        load_c(0, 1)
-        for q in range(4):
+        load_c(0)
+        nc.sync.dma_start(out=rate_rows[0 : R // P, :], in_=rate.rearrange("(m p) -> m p", p=P))
+        load_c(1)
+        for q in range(QUADRANTS):
             nc.sync.dma_start(
-                out=x_scales[32 * q : 32 * q + 4 * PASSES, :].bitcast(I32),
-                in_=infected_scales[:, 4 * q : 4 * q + 4, :].bitcast(I32),
+                out=x_scales[QUADRANT * q : QUADRANT * q + SCALE_ROWS * PASSES, :].bitcast(I32),
+                in_=infected_scales[:, SCALE_ROWS * q : SCALE_ROWS * (q + 1), :].bitcast(I32),
             )
-
-        load_x(0, [0, 1])
-        load_c(1, 0)
-        load_x(1, [0, 1])
-        load_s(0, 0, [0, 1])
-        load_s(0, 1, [0, 1])
-        load_x(2, [0, 1])
-        load_c(1, 1)
-        load_x(3, [0, 1])
-        load_s(0, 0, [2, 3])
-        load_s(0, 1, [2, 3])
-        load_s(1, 0, [0, 1, 2, 3])
-        load_s(1, 1, [0, 1, 2, 3])
+        load_x([0])
+        load_x([1])
+        for k in range(DIRECT):
+            load_susc(0, k, [0, 1])
+        load_x([2, 3])
+        for k in range(DIRECT):
+            load_susc(0, k, [2, 3])
+        for k in range(DIRECT):
+            load_susc(1, k, [0, 1, 2, 3])
 
         ident_bf = keep.tile([P, P], BF16, name="ident_bf")
         make_identity(nc, ident_bf[:])
         outside_rows = keep.tile([P, P], BF16, name="outside_rows")
         nc.gpsimd.memset(outside_rows[:], 0.0)
-        nc.gpsimd.dma_start(out=outside_rows[0 : A // P, :], in_=outside.rearrange("(c p) -> c p", p=P))
+        nc.gpsimd.dma_start(out=outside_rows[0 : A // P, :], in_=outside.rearrange("(m p) -> m p", p=P))
         ident = keep.tile([P, P], F32, name="ident")
         nc.scalar.activation(out=ident[:], in_=ident_bf[:], func=COPY)
 
         c_codes, c_scales, c_grouped = {}, {}, {}
 
-        def interleave_c(h, g, eng, lo, hi):
-            if (h, g) not in c_grouped:
-                c_grouped[h, g] = keep.tile([P, W * PACK], BF16, name="c_grouped_%d_%d" % (h, g), align_bytes=64)
-            dst = c_grouped[h, g][:, PACK * lo : PACK * hi].rearrange("p (c i t) -> p c t i", i=4, t=PACK)
-            src = c_raw[h, g][:, :, lo:hi].rearrange("p t (c i) -> p c t i", i=4)
-            if eng == "v":
-                nc.vector.tensor_copy(out=dst, in_=src)
-            else:
-                nc.scalar.copy(out=dst, in_=src)
+        def interleave_c(h, g):
+            c_grouped[h, g] = keep.tile([P, W * PACK], BF16, name="c_grouped_%d_%d" % (h, g), align_bytes=64)
+            for copy, lo, hi in ((nc.vector.tensor_copy, 0, V_COLS), (nc.scalar.copy, V_COLS, W)):
+                copy(
+                    out=c_grouped[h, g][:, PACK * lo : PACK * hi].rearrange("p (n i t) -> p n t i", i=4, t=PACK),
+                    in_=c_raw[h, g][:, :, lo:hi].rearrange("p t (n i) -> p n t i", i=4),
+                )
 
         def quantize_c(h, g):
             c_codes[h, g] = keep.tile([P, W], U32, name="c_codes_%d_%d" % (h, g), align_bytes=64)
             c_scales[h, g] = keep.tile([P, W], U8, name="c_scales_%d_%d" % (h, g), align_bytes=64)
             nc.vector.quantize_mx(out=c_codes[h, g][:].bitcast(FP8X4), scales=c_scales[h, g][:], in_=c_grouped[h, g][:])
 
-        cols = keep.tile([P, R // P], F32, name="cols")
+        rate_cols = keep.tile([P, R // P], F32, name="rate_cols")
         outside_cols = keep.tile([P, A // P], F32, name="outside_cols")
-        rate_cols = keep.tile([P, R // P], BF16, name="rate_cols")
-        rate_rows = [keep.tile([P, 2 * W], BF16, name="rate_rows_%d" % n) for n in range(CHUNKS // 2)]
-        y_scales = keep.tile([P, A], U8, name="y_scales", align_bytes=64)
-        sums, scaled, turned, y_tiles, rounded, grouped, y_codes = {}, {}, {}, {}, {}, {}, {}
+        rate_cols_bf = keep.tile([P, R // P], BF16, name="rate_cols_bf")
+        rate_spread = [keep.tile([P, 2 * W], BF16, name="rate_spread_%d" % n) for n in range(CHUNKS // 2)]
 
-        def turn_vectors():
-            bank = psum.tile([P, P], BF16, name="vec_ps", tag="u0")
-            nc.tensor.transpose(bank[:], vec_rows[:], ident_bf[:])
-            nc.scalar.copy(out=cols[:], in_=bank[:, 0 : R // P])
+        def turn_rate():
+            bank = psum.tile([P, P], BF16, name="rate_ps", tag="words0")
+            nc.tensor.transpose(bank[:], rate_rows[:], ident_bf[:])
             nc.scalar.copy(out=rate_cols[:], in_=bank[:, 0 : R // P])
+            nc.scalar.copy(out=rate_cols_bf[:], in_=bank[:, 0 : R // P])
 
         def turn_outside():
-            bank = psum.tile([P, P], BF16, name="outside_ps", tag="u0")
+            bank = psum.tile([P, P], BF16, name="outside_ps", tag="words0")
             nc.tensor.transpose(bank[:], outside_rows[:], ident_bf[:])
             nc.scalar.copy(out=outside_cols[:], in_=bank[:, 0 : A // P])
 
         def spread_rate(n, tag):
-            bank = psum.tile([P, 2 * W], BF16, name="rate_ps", tag=tag)
-            for m in range(2 * SUB):
-                col = 2 * SUB * n + m
+            bank = psum.tile([P, 2 * W], BF16, name="spread_ps", tag=tag)
+            for j in range(2 * STRIPS):
+                m = 2 * STRIPS * n + j
                 nc.tensor.transpose(
-                    bank[:, P * m : P * (m + 1)], rate_cols[:, col : col + 1].to_broadcast([P, P]), ident_bf[:]
+                    bank[:, P * j : P * (j + 1)], rate_cols_bf[:, m : m + 1].to_broadcast([P, P]), ident_bf[:]
                 )
-            nc.scalar.copy(out=rate_rows[n][:], in_=bank[:])
+            nc.scalar.copy(out=rate_spread[n][:], in_=bank[:])
+
+        y_scales = keep.tile([P, A], U8, name="y_scales", align_bytes=64)
+        direct_sums, slice_sums, scaled_slices, rated = {}, {}, {}, {}
+        y_tiles, y_runs, rounded, y_grouped, y_codes = {}, {}, {}, {}, {}
+        for run in Y_RUNS:
+            t = keep.tile([P, STRIPS, len(run) * W], F32, name="y_%d" % run[0])
+            y_runs[run[-1]] = (run, t)
+            for n, b in enumerate(run):
+                y_tiles[b] = t[:, :, W * n : W * (n + 1)]
 
         def x_operand(c, g, lo, hi):
-            return x_words[c, g][:, lo:hi].bitcast(FP8X4), x_scales[4 * g :, W * c + lo : W * c + hi]
+            return x_words[c, g][:, lo:hi].bitcast(FP8X4), x_scales[SCALE_ROWS * g :, W * c + lo : W * c + hi]
 
         def c_operand(h, g, lo, hi):
             return c_codes[h, g][:, lo:hi].bitcast(FP8X4), c_scales[h, g][:, lo:hi]
@@ -161,195 +163,176 @@ def tile_contact_infection_pressure_g6_kernel(
 
         def multiply_direct(b, i):
             h, c = divmod(b, CHUNKS)
-            sums[b, "d", i] = psum.tile([P, W], F32, name="sums_d", tag="a%d" % i)
+            direct_sums[b, i] = psum.tile([P, W], F32, name="direct_ps", tag="direct%d" % i)
             for g in range(PASSES):
-                mx_pass(sums[b, "d", i][:], c_operand(h, g, P * i, P * (i + 1)), x_operand(c, g, 0, W), g)
+                mx_pass(direct_sums[b, i][:], c_operand(h, g, P * i, P * (i + 1)), x_operand(c, g, 0, W), g)
 
-        def multiply_turned(b, j, g):
+        def multiply_slice(b, j, out):
             h, c = divmod(b, CHUNKS)
-            mx_pass(sums[b, "t", j], x_operand(c, g, P * j, P * (j + 1)), c_operand(h, g, W // 2, W), g)
+            slice_sums[b, j] = out
+            for g in range(PASSES):
+                mx_pass(out, x_operand(c, g, P * j, P * (j + 1)), c_operand(h, g, P * DIRECT, W), g)
 
-        def scale_turned(b, j):
-            c = b % CHUNKS
-            scaled[b, j] = work.tile([P, W // 2], F32, name="scaled", tag="scaled%d" % j)
-            nc.scalar.activation(
-                out=scaled[b, j][:], in_=sums[b, "t", j], func=COPY, scale=cols[:, SUB * c + j : SUB * c + j + 1]
-            )
+        def scale_slice(b, j):
+            m = STRIPS * (b % CHUNKS) + j
+            scaled_slices[b, j] = work.tile([P, W - P * DIRECT], F32, name="scaled", tag="scaled%d" % j)
+            nc.scalar.activation(out=scaled_slices[b, j][:], in_=slice_sums[b, j], func=COPY, scale=rate_cols[:, m : m + 1])
 
-        def multiply_pair(b, k):
-            bank = psum.tile([P, 2, W // 2], F32, name="sums_t", tag="b%d" % k)
+        def slice_pair(b, k):
+            bank = psum.tile([P, 2, W // 2], F32, name="slices_ps", tag="slices%d" % k)
             for n in range(2):
-                sums[b, "t", 2 * k + n] = bank[:, n, :]
-                for g in range(PASSES):
-                    multiply_turned(b, 2 * k + n, g)
+                multiply_slice(b, 2 * k + n, bank[:, n, :])
             for n in range(2):
-                scale_turned(b, 2 * k + n)
+                scale_slice(b, 2 * k + n)
 
         def scale_direct(b, i):
             c = b % CHUNKS
-            turned[b, i] = work.tile([P, W], F32, name="direct", tag="direct")
+            rated[b, i] = work.tile([P, W], F32, name="rated", tag="rated")
             nc.vector.tensor_tensor(
-                out=turned[b, i][:], in0=sums[b, "d", i][:], in1=rate_rows[c // 2][:, W * (c % 2) : W * (c % 2 + 1)], op=MULT
+                out=rated[b, i][:],
+                in0=direct_sums[b, i][:],
+                in1=rate_spread[c // 2][:, W * (c % 2) : W * (c % 2 + 1)],
+                op=MULT,
             )
 
         def turn(b, i):
-            turned[b, i] = psum.tile([P, W], F32, name="turned", tag="t%d" % (i % 2))
-            for j in range(SUB):
+            rated[b, i] = psum.tile([P, W], F32, name="turned_ps", tag="turned%d" % (i - DIRECT))
+            for j in range(STRIPS):
                 nc.tensor.transpose(
-                    turned[b, i][:, P * j : P * (j + 1)], scaled[b, j][:, P * (i - 2) : P * (i - 1)], ident[:]
+                    rated[b, i][:, P * j : P * (j + 1)],
+                    scaled_slices[b, j][:, P * (i - DIRECT) : P * (i - DIRECT + 1)],
+                    ident[:],
                 )
+
+        def pressure(b, i, out, in0, in1):
+            m = STRIPS * (b // CHUNKS) + i
+            nc.vector.scalar_tensor_tensor(
+                out=out, in0=in0, scalar=outside_cols[:, m : m + 1], in1=in1, op0=ADD, op1=MULT
+            )
 
         def finish(b, i):
             h, c = divmod(b, CHUNKS)
-            if b not in y_tiles:
-                wide = work.tile([P, SUB, 2 * W], F32, name="y", tag="y", bufs=3)
-                y_tiles[b], y_tiles[b + 1], y_tiles[b, b + 1] = wide[:, :, :W], wide[:, :, W:], wide
-            nc.vector.scalar_tensor_tensor(
-                out=y_tiles[b][:, i, :],
-                in0=turned[b, i][:],
-                scalar=outside_cols[:, SUB * h + i : SUB * h + i + 1],
-                in1=susc[h, c, i],
-                op0=ADD,
-                op1=MULT,
+            pressure(b, i, y_tiles[b][:, i, :], rated[b, i][:], susc[h, c, i])
+
+        def by_pairs(natural):
+            return natural.rearrange("a (p u e) -> a u p e", u=2, e=2)
+
+        def new_rounded(b, i):
+            rounded[b, i] = work.tile([P, W], BF16, name="rounded", tag="rounded%d" % i)
+            return rounded[b, i][:].rearrange("a (u p e) -> a u p e", u=2, e=2)
+
+        def round_on_scalar(b, i):
+            nc.scalar.copy(out=new_rounded(b, i), in_=by_pairs(y_tiles[b][:, i, :]))
+
+        def round_on_gpsimd(b, i):
+            nc.gpsimd.tensor_scalar(
+                out=new_rounded(b, i), in0=by_pairs(y_tiles[b][:, i, :]), scalar1=1.0, scalar2=-0.0, op0=MULT, op1=ADD
             )
 
         def finish_rounded(b, i):
             h, c = divmod(b, CHUNKS)
-            rounded[b, i] = work.tile([P, W], BF16, name="rounded", tag="rounded%d" % i)
+            out = new_rounded(b, i)
             for u in range(2):
-                nc.vector.scalar_tensor_tensor(
-                    out=rounded[b, i][:].rearrange("a (u p e) -> a u p e", u=2, e=2)[:, u],
-                    in0=turned[b, i][:].rearrange("a (p u e) -> a u p e", u=2, e=2)[:, u],
-                    scalar=outside_cols[:, SUB * h + i : SUB * h + i + 1],
-                    in1=susc[h, c, i].rearrange("a (p u e) -> a u p e", u=2, e=2)[:, u],
-                    op0=ADD,
-                    op1=MULT,
-                )
+                pressure(b, i, out[:, u], by_pairs(rated[b, i][:])[:, u], by_pairs(susc[h, c, i])[:, u])
 
-        def round_y(b, i, copy):
-            rounded[b, i] = work.tile([P, W], BF16, name="rounded", tag="rounded%d" % i)
-            copy(
-                out=rounded[b, i][:].rearrange("a (u p e) -> a u p e", u=2, e=2),
-                in_=y_tiles[b][:, i, :].rearrange("a (p u e) -> a u p e", u=2, e=2),
-            )
-
-        def turn_words(b, subs, tag, copy):
-            if b not in grouped:
-                grouped[b] = work.tile([P, W * PACK], BF16, name="grouped", tag="grouped", bufs=3, align_bytes=64)
-            bank = psum.tile([P, len(subs), 2, P], F32, name="words_ps", tag=tag)
-            for n, i in enumerate(subs):
-                words = rounded[b, i][:].bitcast(F32)
+        def turn_words(b, k):
+            if k == 0:
+                y_grouped[b] = work.tile([P, W * PACK], BF16, name="y_grouped", tag="y_grouped", bufs=3, align_bytes=64)
+            bank = psum.tile([P, 2, 2, P], F32, name="words_ps", tag="words%d" % k)
+            for n in range(2):
+                words = rounded[b, DIRECT * n + k][:].bitcast(F32)
                 for u in range(2):
                     nc.tensor.transpose(bank[:, n, u, :], words[:, P * u : P * (u + 1)], ident[:])
-            dst = grouped[b][:].bitcast(F32).rearrange("p (i a u) -> p i a u", i=SUB, u=2)
-            copy(out=dst[:, subs[0] : subs[-1] + 1 : 2, :, :], in_=bank[:].rearrange("p n u a -> p n a u"))
+            dst = y_grouped[b][:].bitcast(F32).rearrange("p (i a u) -> p i a u", i=STRIPS, u=2)
+            nc.scalar.copy(out=dst[:, k::DIRECT, :, :], in_=bank[:].rearrange("p n u a -> p n a u"))
 
         def quantize_y(b, lo, hi):
             h, c = divmod(b, CHUNKS)
-            if b not in y_codes:
+            if lo == 0:
                 y_codes[b] = work.tile([P, W], U32, name="y_codes", tag="y_codes", bufs=4, align_bytes=64)
             nc.vector.quantize_mx(
                 out=y_codes[b][:, P * lo : P * hi].bitcast(FP8X4),
-                scales=y_scales[4 * c :, W * h + P * lo : W * h + P * hi],
-                in_=grouped[b][:, W * lo : W * hi],
+                scales=y_scales[SCALE_ROWS * c :, W * h + P * lo : W * h + P * hi],
+                in_=y_grouped[b][:, W * lo : W * hi],
             )
 
-        def store_codes(b, lo, hi):
+        def store_codes(b):
             h, c = divmod(b, CHUNKS)
-            dst = out_1[c].rearrange("p m t -> p (m t)")[:, PACK * (W * h + P * lo) : PACK * (W * h + P * hi)]
-            nc.sync.dma_start(out=dst.bitcast(I32), in_=y_codes[b][:, P * lo : P * hi].bitcast(I32))
+            dst = out_1[c].rearrange("p m t -> p (m t)")[:, PACK * W * h : PACK * W * (h + 1)]
+            nc.sync.dma_start(out=dst.bitcast(I32), in_=y_codes[b][:].bitcast(I32))
 
-        def store_y(first, last_b, subs):
-            h, c = divmod(first, CHUNKS)
-            dst = out_0[W * h : W * (h + 1), W * c : W * (c + 1 + last_b - first)].rearrange("(i p) r -> p i r", p=P)
-            src = y_tiles[first] if first == last_b else y_tiles[first, last_b]
-            nc.sync.dma_start(out=dst[:, subs, :], in_=src[:, subs, :])
+        def store_y(b, strips):
+            if b in y_runs:
+                run, t = y_runs[b]
+                h, c = divmod(run[0], CHUNKS)
+                dst = out_0[W * h : W * (h + 1), W * c : W * (c + len(run))].rearrange("(i p) r -> p i r", p=P)
+                nc.sync.dma_start(out=dst[:, strips, :], in_=t[:, strips, :])
 
-        def on_gpsimd(out, in_):
-            nc.gpsimd.tensor_scalar(out=out, in0=in_, scalar1=1.0, scalar2=0.0, op0=MULT, op1=ADD)
-
-        on_vector, on_scalar = nc.vector.tensor_copy, nc.scalar.copy
-
-        interleave_c(0, 0, "v", 0, V_COLS)
-        interleave_c(0, 0, "s", V_COLS, W)
-        turn_vectors()
+        interleave_c(0, 0)
+        turn_rate()
+        interleave_c(1, 0)
         quantize_c(0, 0)
-        interleave_c(0, 1, "v", 0, V_COLS)
-        interleave_c(0, 1, "s", V_COLS, W)
-        spread_rate(0, "u1")
-        spread_rate(1, "t1")
-        turn_outside()
-        quantize_c(0, 1)
-        multiply_direct(0, 0)
-        for j, tag in enumerate(["b0", "b1", "t0", "t1"]):
-            bank = psum.tile([P, W // 2], F32, name="sums_0", tag=tag)
-            sums[0, "t", j] = bank[:]
-            for g in range(PASSES):
-                multiply_turned(0, j, g)
-            scale_turned(0, j)
-        scale_direct(0, 0)
-        interleave_c(1, 0, "v", 0, W)
         quantize_c(1, 0)
+        interleave_c(0, 1)
+        spread_rate(0, "words1")
+        quantize_c(0, 1)
+        interleave_c(1, 1)
+        spread_rate(1, "turned1")
+        turn_outside()
+        multiply_direct(0, 0)
+        for j, tag in enumerate(["slices0", "slices1", "turned0", "turned1"]):
+            bank = psum.tile([P, W // 2], F32, name="first_slices_ps", tag=tag)
+            multiply_slice(0, j, bank[:])
+            scale_slice(0, j)
+        quantize_c(1, 1)
+        scale_direct(0, 0)
 
-        def store_pair(b, k):
-            if b >= 4:
-                store_y(b, b, slice(k, SUB, 2))
-            elif b % 2 == 1:
-                store_y(b - 1, b, slice(k, SUB, 2))
-
-        last = 2 * BLOCKS - 1
-        for s in range(last):
-            b, k = divmod(s, 2)
-            b1, k1 = divmod(s - 1, 2)
-            multiply_direct(*divmod(s + 1, 2))
+        for s in range(DIRECT * BLOCKS - 1):
+            b, k = divmod(s, DIRECT)
+            multiply_direct(*divmod(s + 1, DIRECT))
             if b + 1 < BLOCKS:
-                multiply_pair(b + 1, k)
+                slice_pair(b + 1, k)
             if s > 0:
+                b_before, k_before = divmod(s - 1, DIRECT)
                 scale_direct(b, k)
-                finish(b1, 2 + k1)
-                store_pair(b1, k1)
-                round_y(b1, 2 + k1, on_scalar)
-            turn(b, 2 + k)
-            if s >= 2:
-                turn_words(b - 1, [k, 2 + k], "u%d" % k, on_scalar)
-            if s == 4:
-                interleave_c(1, 1, "v", 0, W // 2)
-            if s in (2, 3):
-                interleave_c(1, 1, "s", P * s, P * (s + 1))
-            if s == 5:
-                quantize_c(1, 1)
-            if s >= 5 and k == 1:
-                quantize_y(b - 2, 0, SUB)
-                store_codes(b - 2, 0, SUB)
+                finish(b_before, DIRECT + k_before)
+                store_y(b_before, slice(k_before, STRIPS, DIRECT))
+                round_on_scalar(b_before, DIRECT + k_before)
+            turn(b, DIRECT + k)
+            if b >= 1:
+                turn_words(b - 1, k)
+            if b >= 2 and k == DIRECT - 1:
+                quantize_y(b - 2, 0, STRIPS)
+                store_codes(b - 2)
             finish(b, k)
-            round_y(b, k, on_gpsimd)
+            round_on_gpsimd(b, k)
 
         b = BLOCKS - 1
         turn(b, 3)
         finish(b, 2)
-        store_pair(b, 0)
-        round_y(b, 2, on_scalar)
-        turn_words(b - 1, [1, 3], "u1", on_scalar)
-        scale_direct(b, 1)
+        store_y(b, slice(0, STRIPS, DIRECT))
+        round_on_gpsimd(b, 2)
         finish(b, 3)
-        store_y(b, b, slice(3, 4))
-        round_y(b, 3, on_scalar)
-        turn_words(b, [0, 2], "u0", on_scalar)
+        store_y(b, slice(3, 4))
+        turn_words(b - 1, 1)
+        round_on_scalar(b, 3)
+        scale_direct(b, 1)
+        quantize_y(b - 2, 0, STRIPS)
+        store_codes(b - 2)
         finish_rounded(b, 1)
+        turn_words(b, 0)
+        quantize_y(b - 1, 0, STRIPS)
+        store_codes(b - 1)
         finish(b, 1)
-        store_y(b, b, slice(1, 2))
-        turn_words(b, [1, 3], "u1", on_scalar)
-        quantize_y(b - 2, 0, SUB)
-        store_codes(b - 2, 0, SUB)
-        quantize_y(b - 1, 0, SUB)
-        store_codes(b - 1, 0, SUB)
-        quantize_y(b, 0, 1)
-        quantize_y(b, 2, 3)
-        quantize_y(b, 1, 2)
-        quantize_y(b, 3, 4)
-        store_codes(b, 0, SUB)
+        store_y(b, slice(1, 2))
+        turn_words(b, 1)
+        for k in range(DIRECT):
+            for i in range(k, STRIPS, DIRECT):
+                quantize_y(b, i, i + 1)
+        store_codes(b)
 
-        for q in range(4):
+        for q in range(QUADRANTS):
             nc.scalar.dma_start(
-                out=out_2[:, 4 * q : 4 * q + 4, :].bitcast(I32), in_=y_scales[32 * q : 32 * q + 4 * CHUNKS, :].bitcast(I32)
+                out=out_2[:, SCALE_ROWS * q : SCALE_ROWS * (q + 1), :].bitcast(I32),
+                in_=y_scales[QUADRANT * q : QUADRANT * q + SCALE_ROWS * CHUNKS, :].bitcast(I32),
             )

from contextlib import ExitStack

import concourse.mybir as mybir
from concourse.masks import make_identity

F32 = mybir.dt.float32
BF16 = mybir.dt.bfloat16
I32 = mybir.dt.int32
U32 = mybir.dt.uint32
U8 = mybir.dt.uint8
FP8X4 = mybir.dt.float8_e4m3fn_x4
COPY = mybir.ActivationFunctionType.Copy
ADD = mybir.AluOpType.add
MULT = mybir.AluOpType.mult

A, R = 1024, 2048
P = 128
PACK = 4
QUADRANTS, QUADRANT = 4, 32
SCALE_ROWS = 4
W = 512
STRIPS = W // P
DIRECT = STRIPS // 2
PASSES = A // W
HALVES = A // W
CHUNKS = R // W
BLOCKS = HALVES * CHUNKS
V_COLS = 352
Y_RUNS = [[b, b + 1] for b in range(0, CHUNKS, 2)] + [[b] for b in range(CHUNKS, BLOCKS)]
FLOPS = 2 * A * A * R


def tile_contact_infection_pressure_g6_kernel(
    tc, infected_words, infected_scales, contact, rate, outside, susceptibility, out_0, out_1, out_2
):
    nc = tc.nc
    with ExitStack() as ctx:
        keep = ctx.enter_context(tc.tile_pool(name="keep", bufs=1))
        work = ctx.enter_context(tc.tile_pool(name="work", bufs=2))
        psum = ctx.enter_context(tc.psum_pool(name="psum", bufs=1))
        ctx.enter_context(tc.manual_schedule())

        rate_rows = keep.tile([P, P], BF16, name="rate_rows")
        nc.vector.memset(rate_rows[:], 0.0)
        x_scales = keep.tile([P, R], U8, name="x_scales", align_bytes=64)
        nc.vector.memset(x_scales[:].bitcast(I32), 0)

        c_raw, x_words, susc = {}, {}, {}

        def load_c(g):
            t = keep.tile([P, PACK, A], BF16, name="c_raw_%d" % g)
            nc.sync.dma_start(out=t[:], in_=contact[W * g : W * (g + 1), :].rearrange("(p j) a -> p j a", j=PACK))
            for h in range(HALVES):
                c_raw[h, g] = t[:, :, W * h : W * (h + 1)]

        def load_x(chunks):
            t = keep.tile([P, PASSES, len(chunks) * W], U32, name="x_words_%d" % chunks[0], align_bytes=64)
            src = infected_words.rearrange("g p n t -> p g (n t)")[:, :, PACK * W * chunks[0] : PACK * W * (chunks[-1] + 1)]
            nc.sync.dma_start(out=t[:].bitcast(I32), in_=src.bitcast(I32))
            for g in range(PASSES):
                for n, c in enumerate(chunks):
                    x_words[c, g] = t[:, g, W * n : W * (n + 1)]

        def load_susc(h, k, chunks):
            t = keep.tile([P, 2, len(chunks) * W], BF16, name="susc_%d_%d_%d" % (h, k, chunks[0]))
            rows = susceptibility[W * h : W * (h + 1), W * chunks[0] : W * (chunks[-1] + 1)]
            nc.sync.dma_start(out=t[:], in_=rows.rearrange("(i p) r -> p i r", p=P)[:, k::DIRECT, :])
            for n, c in enumerate(chunks):
                susc[h, c, k] = t[:, 0, W * n : W * (n + 1)]
                susc[h, c, DIRECT + k] = t[:, 1, W * n : W * (n + 1)]

        load_c(0)
        nc.sync.dma_start(out=rate_rows[0 : R // P, :], in_=rate.rearrange("(m p) -> m p", p=P))
        load_c(1)
        for q in range(QUADRANTS):
            nc.sync.dma_start(
                out=x_scales[QUADRANT * q : QUADRANT * q + SCALE_ROWS * PASSES, :].bitcast(I32),
                in_=infected_scales[:, SCALE_ROWS * q : SCALE_ROWS * (q + 1), :].bitcast(I32),
            )
        load_x([0])
        load_x([1])
        for k in range(DIRECT):
            load_susc(0, k, [0, 1])
        load_x([2, 3])
        for k in range(DIRECT):
            load_susc(0, k, [2, 3])
        for k in range(DIRECT):
            load_susc(1, k, [0, 1, 2, 3])

        ident_bf = keep.tile([P, P], BF16, name="ident_bf")
        make_identity(nc, ident_bf[:])
        outside_rows = keep.tile([P, P], BF16, name="outside_rows")
        nc.gpsimd.memset(outside_rows[:], 0.0)
        nc.gpsimd.dma_start(out=outside_rows[0 : A // P, :], in_=outside.rearrange("(m p) -> m p", p=P))
        ident = keep.tile([P, P], F32, name="ident")
        nc.scalar.activation(out=ident[:], in_=ident_bf[:], func=COPY)

        c_codes, c_scales, c_grouped = {}, {}, {}

        def interleave_c(h, g):
            c_grouped[h, g] = keep.tile([P, W * PACK], BF16, name="c_grouped_%d_%d" % (h, g), align_bytes=64)
            for copy, lo, hi in ((nc.vector.tensor_copy, 0, V_COLS), (nc.scalar.copy, V_COLS, W)):
                copy(
                    out=c_grouped[h, g][:, PACK * lo : PACK * hi].rearrange("p (n i t) -> p n t i", i=4, t=PACK),
                    in_=c_raw[h, g][:, :, lo:hi].rearrange("p t (n i) -> p n t i", i=4),
                )

        def quantize_c(h, g):
            c_codes[h, g] = keep.tile([P, W], U32, name="c_codes_%d_%d" % (h, g), align_bytes=64)
            c_scales[h, g] = keep.tile([P, W], U8, name="c_scales_%d_%d" % (h, g), align_bytes=64)
            nc.vector.quantize_mx(out=c_codes[h, g][:].bitcast(FP8X4), scales=c_scales[h, g][:], in_=c_grouped[h, g][:])

        rate_cols = keep.tile([P, R // P], F32, name="rate_cols")
        outside_cols = keep.tile([P, A // P], F32, name="outside_cols")
        rate_cols_bf = keep.tile([P, R // P], BF16, name="rate_cols_bf")
        rate_spread = [keep.tile([P, 2 * W], BF16, name="rate_spread_%d" % n) for n in range(CHUNKS // 2)]

        def turn_rate():
            bank = psum.tile([P, P], BF16, name="rate_ps", tag="words0")
            nc.tensor.transpose(bank[:], rate_rows[:], ident_bf[:])
            nc.scalar.copy(out=rate_cols[:], in_=bank[:, 0 : R // P])
            nc.scalar.copy(out=rate_cols_bf[:], in_=bank[:, 0 : R // P])

        def turn_outside():
            bank = psum.tile([P, P], BF16, name="outside_ps", tag="words0")
            nc.tensor.transpose(bank[:], outside_rows[:], ident_bf[:])
            nc.scalar.copy(out=outside_cols[:], in_=bank[:, 0 : A // P])

        def spread_rate(n, tag):
            bank = psum.tile([P, 2 * W], BF16, name="spread_ps", tag=tag)
            for j in range(2 * STRIPS):
                m = 2 * STRIPS * n + j
                nc.tensor.transpose(
                    bank[:, P * j : P * (j + 1)], rate_cols_bf[:, m : m + 1].to_broadcast([P, P]), ident_bf[:]
                )
            nc.scalar.copy(out=rate_spread[n][:], in_=bank[:])

        y_scales = keep.tile([P, A], U8, name="y_scales", align_bytes=64)
        direct_sums, slice_sums, scaled_slices, rated = {}, {}, {}, {}
        y_tiles, y_runs, rounded, y_grouped, y_codes = {}, {}, {}, {}, {}
        for run in Y_RUNS:
            t = keep.tile([P, STRIPS, len(run) * W], F32, name="y_%d" % run[0])
            y_runs[run[-1]] = (run, t)
            for n, b in enumerate(run):
                y_tiles[b] = t[:, :, W * n : W * (n + 1)]

        def x_operand(c, g, lo, hi):
            return x_words[c, g][:, lo:hi].bitcast(FP8X4), x_scales[SCALE_ROWS * g :, W * c + lo : W * c + hi]

        def c_operand(h, g, lo, hi):
            return c_codes[h, g][:, lo:hi].bitcast(FP8X4), c_scales[h, g][:, lo:hi]

        def mx_pass(out, stationary, moving, g):
            nc.tensor.matmul_mx(
                out=out,
                lhsT=stationary[0],
                lhsT_scale=stationary[1],
                rhs=moving[0],
                rhs_scale=moving[1],
                start=(g == 0),
                stop=(g == PASSES - 1),
            )

        def multiply_direct(b, i):
            h, c = divmod(b, CHUNKS)
            direct_sums[b, i] = psum.tile([P, W], F32, name="direct_ps", tag="direct%d" % i)
            for g in range(PASSES):
                mx_pass(direct_sums[b, i][:], c_operand(h, g, P * i, P * (i + 1)), x_operand(c, g, 0, W), g)

        def multiply_slice(b, j, out):
            h, c = divmod(b, CHUNKS)
            slice_sums[b, j] = out
            for g in range(PASSES):
                mx_pass(out, x_operand(c, g, P * j, P * (j + 1)), c_operand(h, g, P * DIRECT, W), g)

        def scale_slice(b, j):
            m = STRIPS * (b % CHUNKS) + j
            scaled_slices[b, j] = work.tile([P, W - P * DIRECT], F32, name="scaled", tag="scaled%d" % j)
            nc.scalar.activation(out=scaled_slices[b, j][:], in_=slice_sums[b, j], func=COPY, scale=rate_cols[:, m : m + 1])

        def slice_pair(b, k):
            bank = psum.tile([P, 2, W // 2], F32, name="slices_ps", tag="slices%d" % k)
            for n in range(2):
                multiply_slice(b, 2 * k + n, bank[:, n, :])
            for n in range(2):
                scale_slice(b, 2 * k + n)

        def scale_direct(b, i):
            c = b % CHUNKS
            rated[b, i] = work.tile([P, W], F32, name="rated", tag="rated")
            nc.vector.tensor_tensor(
                out=rated[b, i][:],
                in0=direct_sums[b, i][:],
                in1=rate_spread[c // 2][:, W * (c % 2) : W * (c % 2 + 1)],
                op=MULT,
            )

        def turn(b, i):
            rated[b, i] = psum.tile([P, W], F32, name="turned_ps", tag="turned%d" % (i - DIRECT))
            for j in range(STRIPS):
                nc.tensor.transpose(
                    rated[b, i][:, P * j : P * (j + 1)],
                    scaled_slices[b, j][:, P * (i - DIRECT) : P * (i - DIRECT + 1)],
                    ident[:],
                )

        def pressure(b, i, out, in0, in1):
            m = STRIPS * (b // CHUNKS) + i
            nc.vector.scalar_tensor_tensor(
                out=out, in0=in0, scalar=outside_cols[:, m : m + 1], in1=in1, op0=ADD, op1=MULT
            )

        def finish(b, i):
            h, c = divmod(b, CHUNKS)
            pressure(b, i, y_tiles[b][:, i, :], rated[b, i][:], susc[h, c, i])

        def by_pairs(natural):
            return natural.rearrange("a (p u e) -> a u p e", u=2, e=2)

        def new_rounded(b, i):
            rounded[b, i] = work.tile([P, W], BF16, name="rounded", tag="rounded%d" % i)
            return rounded[b, i][:].rearrange("a (u p e) -> a u p e", u=2, e=2)

        def round_on_scalar(b, i):
            nc.scalar.copy(out=new_rounded(b, i), in_=by_pairs(y_tiles[b][:, i, :]))

        def round_on_gpsimd(b, i):
            nc.gpsimd.tensor_scalar(
                out=new_rounded(b, i), in0=by_pairs(y_tiles[b][:, i, :]), scalar1=1.0, scalar2=-0.0, op0=MULT, op1=ADD
            )

        def finish_rounded(b, i):
            h, c = divmod(b, CHUNKS)
            out = new_rounded(b, i)
            for u in range(2):
                pressure(b, i, out[:, u], by_pairs(rated[b, i][:])[:, u], by_pairs(susc[h, c, i])[:, u])

        def turn_words(b, k):
            if k == 0:
                y_grouped[b] = work.tile([P, W * PACK], BF16, name="y_grouped", tag="y_grouped", bufs=3, align_bytes=64)
            bank = psum.tile([P, 2, 2, P], F32, name="words_ps", tag="words%d" % k)
            for n in range(2):
                words = rounded[b, DIRECT * n + k][:].bitcast(F32)
                for u in range(2):
                    nc.tensor.transpose(bank[:, n, u, :], words[:, P * u : P * (u + 1)], ident[:])
            dst = y_grouped[b][:].bitcast(F32).rearrange("p (i a u) -> p i a u", i=STRIPS, u=2)
            nc.scalar.copy(out=dst[:, k::DIRECT, :, :], in_=bank[:].rearrange("p n u a -> p n a u"))

        def quantize_y(b, lo, hi):
            h, c = divmod(b, CHUNKS)
            if lo == 0:
                y_codes[b] = work.tile([P, W], U32, name="y_codes", tag="y_codes", bufs=4, align_bytes=64)
            nc.vector.quantize_mx(
                out=y_codes[b][:, P * lo : P * hi].bitcast(FP8X4),
                scales=y_scales[SCALE_ROWS * c :, W * h + P * lo : W * h + P * hi],
                in_=y_grouped[b][:, W * lo : W * hi],
            )

        def store_codes(b):
            h, c = divmod(b, CHUNKS)
            dst = out_1[c].rearrange("p m t -> p (m t)")[:, PACK * W * h : PACK * W * (h + 1)]
            nc.sync.dma_start(out=dst.bitcast(I32), in_=y_codes[b][:].bitcast(I32))

        def store_y(b, strips):
            if b in y_runs:
                run, t = y_runs[b]
                h, c = divmod(run[0], CHUNKS)
                dst = out_0[W * h : W * (h + 1), W * c : W * (c + len(run))].rearrange("(i p) r -> p i r", p=P)
                nc.sync.dma_start(out=dst[:, strips, :], in_=t[:, strips, :])

        interleave_c(0, 0)
        turn_rate()
        interleave_c(1, 0)
        quantize_c(0, 0)
        quantize_c(1, 0)
        interleave_c(0, 1)
        spread_rate(0, "words1")
        quantize_c(0, 1)
        interleave_c(1, 1)
        spread_rate(1, "turned1")
        turn_outside()
        multiply_direct(0, 0)
        for j, tag in enumerate(["slices0", "slices1", "turned0", "turned1"]):
            bank = psum.tile([P, W // 2], F32, name="first_slices_ps", tag=tag)
            multiply_slice(0, j, bank[:])
            scale_slice(0, j)
        quantize_c(1, 1)
        scale_direct(0, 0)

        for s in range(DIRECT * BLOCKS - 1):
            b, k = divmod(s, DIRECT)
            multiply_direct(*divmod(s + 1, DIRECT))
            if b + 1 < BLOCKS:
                slice_pair(b + 1, k)
            if s > 0:
                b_before, k_before = divmod(s - 1, DIRECT)
                scale_direct(b, k)
                finish(b_before, DIRECT + k_before)
                store_y(b_before, slice(k_before, STRIPS, DIRECT))
                round_on_scalar(b_before, DIRECT + k_before)
            turn(b, DIRECT + k)
            if b >= 1:
                turn_words(b - 1, k)
            if b >= 2 and k == DIRECT - 1:
                quantize_y(b - 2, 0, STRIPS)
                store_codes(b - 2)
            finish(b, k)
            round_on_gpsimd(b, k)

        b = BLOCKS - 1
        turn(b, 3)
        finish(b, 2)
        store_y(b, slice(0, STRIPS, DIRECT))
        round_on_gpsimd(b, 2)
        finish(b, 3)
        store_y(b, slice(3, 4))
        turn_words(b - 1, 1)
        round_on_scalar(b, 3)
        scale_direct(b, 1)
        quantize_y(b - 2, 0, STRIPS)
        store_codes(b - 2)
        finish_rounded(b, 1)
        turn_words(b, 0)
        quantize_y(b - 1, 0, STRIPS)
        store_codes(b - 1)
        finish(b, 1)
        store_y(b, slice(1, 2))
        turn_words(b, 1)
        for k in range(DIRECT):
            for i in range(k, STRIPS, DIRECT):
                quantize_y(b, i, i + 1)
        store_codes(b)

        for q in range(QUADRANTS):
            nc.scalar.dma_start(
                out=out_2[:, SCALE_ROWS * q : SCALE_ROWS * (q + 1), :].bitcast(I32),
                in_=y_scales[QUADRANT * q : QUADRANT * q + SCALE_ROWS * CHUNKS, :].bitcast(I32),
            )
